import numpy as np, ml_dtypes
CORES = [31,71,111]
N = 3
import mx_ref
NC, G = 128, 4
C = np.float32(0.00048828125)
BF = ml_dtypes.bfloat16
def cut(t, i, w=512):
    return t[:, w * i:w * i + w]
def tile(rs):
    return np.stack(rs, axis=2).reshape(128, -1).astype(BF)
def layer(w, X):
    out = []
    for i in range(G):
        for t in range(len(X)):
            p = mx_ref.matmul(mx_ref.quantize(cut(w, len(X) * i + t)), X[t])
            z = p if t == 0 else z + p
        out.append(z)
    return out
def gate(U, V):
    return [(np.maximum(u, 0) * v) * C for u, v in zip(U, V)]
def setup_inputs(rng):
    def f(*shape):
        return mx_ref.flush((rng.standard_normal(shape, dtype=np.float32) * np.exp2(rng.integers(-2, 3, shape[:-1] + (1,)))).astype(BF))
    return {"x": f(N, 128, 4 * NC), "u": f(N, 128, G * 512), "v": f(N, 128, G * 512), "w2": f(N, 128, 512)}
def setup_inputs_blocks(rng):
    d = setup_inputs(rng)
    for k in ("x", "u", "v", "w2"): d[k] = mx_ref.spread(d[k], rng, 4)
    return d
def setup_inputs_wide(rng):
    d = setup_inputs(rng)
    for k in ("x", "u", "v", "w2"): d[k] = mx_ref.flush((d[k].astype(np.float32) * np.exp2(rng.integers(-5, 6, (N, 1, 1))).astype(np.float32)).astype(BF))
    return d
def setup_inputs_zeros(rng):
    d = setup_inputs(rng); v = d["x"].reshape(N, 128, -1, 4).copy()
    v[np.broadcast_to((rng.random((N, 1, v.shape[2], 1)) < 0.33), v.shape)] = 0
    d["x"] = v.reshape(d["x"].shape)
    return d
def reference(x, u, v, w2):
    h = np.zeros((N, 128, 4 * NC), BF)
    for j in range(N):
        X = [mx_ref.quantize(x[j])]
        h[j] = tile(gate(layer(u[j], X), layer(v[j], X)))
    H = [mx_ref.quantize(h[j]) for j in range(N)]
    y = np.zeros((N, 128, N * NC), np.float32)
    for r in range(N):
        qw = mx_ref.quantize(w2[r])
        for j in range(N):
            y[r][:, NC * j:NC * j + NC] = mx_ref.matmul(qw, H[j])
    return {"y": y}

@@ -1,0 +1,130 @@
+from concourse.bass import DstId, RemoteDMATransfer
+from concourse.mybir import dt, AluOpType, ActivationFunctionType
+
+NR = 3
+NC = 128
+G = 4
+TW = 4 * NC
+BANK = 512
+C = 0.00048828125
+
+SCRATCH = {
+    "xb": ("sbuf", [128, TW], "bfloat16"),
+    "ub": ("sbuf", [128, G * TW], "bfloat16"),
+    "vb": ("sbuf", [128, G * TW], "bfloat16"),
+    "wb": ("sbuf", [128, TW], "bfloat16"),
+    "hb": ("sbuf", [128, TW], "bfloat16"),
+    "xq": ("sbuf", [128, NC], "float8_e4m3fn_x4"), "xs": ("sbuf", [128, NC], "uint8"),
+    "uq": ("sbuf", [128, G * NC], "float8_e4m3fn_x4"), "us": ("sbuf", [128, G * NC], "uint8"),
+    "vq": ("sbuf", [128, G * NC], "float8_e4m3fn_x4"), "vs": ("sbuf", [128, G * NC], "uint8"),
+    "wq": ("sbuf", [128, NC], "float8_e4m3fn_x4"), "ws": ("sbuf", [128, NC], "uint8"),
+    "hq": ("sbuf", [128, NR * NC], "float8_e4m3fn_x4"), "hs": ("sbuf", [128, NR * NC], "uint8"),
+    "ru": ("sbuf", [128, G * NC], "float32"),
+    "yb": ("sbuf", [128, NR * NC], "float32"),
+    "pu": ("psum", [128, G * BANK], "float32"),
+    "pv": ("psum", [128, G * BANK], "float32"),
+}
+SEMAPHORES = (["lx", "lu", "lva", "lvb", "lw", "qx", "qw", "qh", "th", "sent"]
+              + ["%s%d" % (k, b) for k in ("qu", "qv", "mu", "mv", "ru") for b in range(G)]
+              + ["%s%d" % (k, j) for k in ("arr", "my", "cy", "st") for j in range(NR)])
+
+
+def cols(t, i, w):
+    return t[:, w * i:w * i + w]
+
+
+def rank_program(g, core, T, topo):
+    r = T.rank_of(core)
+    if r is None:
+        return
+    S = T.sem
+    n = len(T.cores)
+    sync, scal, vec, ten = g.sync, g.scalar, g.vector, g.tensor
+    dests = [(r + k) % n for k in range(1, n)]
+    senders = [(r - k) % n for k in range(1, n)]
+    head = (G - 1) * TW
+
+    scal.dma_start(T.ub[:], T.u[:]).then_inc(S.lu, 16)
+    sync.dma_start(T.xb[:], T.x[:]).then_inc(S.lx, 16)
+    sync.dma_start(T.vb[:, 0:head], T.v[:, 0:head]).then_inc(S.lva, 16)
+    sync.dma_start(T.vb[:, head:G * TW], T.v[:, head:G * TW]).then_inc(S.lvb, 16)
+    scal.wait_ge(S.lu, 16)
+    scal.dma_start(T.wb[:], T.w2[:]).then_inc(S.lw, 16)
+
+    def pack_v(b):
+        vec.quantize_mx(cols(T.vq, b, NC), cols(T.vs, b, NC), cols(T.vb, b, TW)).then_inc(S["qv%d" % b], 1)
+
+    def gate(b):
+        vec.wait_ge(S["ru%d" % b], 1)
+        vec.wait_ge(S["mv%d" % b], 1)
+        vec.tensor_tensor(T.hb[:, b:TW:G], cols(T.ru, b, NC), T.pv[:, BANK * b:BANK * b + NC],
+                          AluOpType.mult).then_inc(S.th, 1)
+
+    vec.wait_ge(S.lx, 16)
+    vec.quantize_mx(T.xq[:], T.xs[:], T.xb[:]).then_inc(S.qx, 1)
+    vec.wait_ge(S.lu, 16)
+    for b in range(G):
+        vec.quantize_mx(cols(T.uq, b, NC), cols(T.us, b, NC), cols(T.ub, b, TW)).then_inc(S["qu%d" % b], 1)
+    vec.wait_ge(S.lva, 16)
+    for b in range(G - 1):
+        pack_v(b)
+    for b in range(G - 2):
+        gate(b)
+    vec.wait_ge(S.lvb, 16)
+    pack_v(G - 1)
+    gate(G - 2)
+    gate(G - 1)
+    vec.wait_ge(S.th, G)
+    vec.quantize_mx(cols(T.hq, r, NC), cols(T.hs, r, NC), T.hb[:]).then_inc(S.qh, 1)
+    vec.wait_ge(S.lw, 16)
+    vec.quantize_mx(T.wq[:], T.ws[:], T.wb[:]).then_inc(S.qw, 1)
+
+    ten.wait_ge(S.qx, 1)
+    for q, s, p, ready, done in ((T.uq, T.us, T.pu, "qu%d", "mu%d"), (T.vq, T.vs, T.pv, "qv%d", "mv%d")):
+        for b in range(G):
+            ten.wait_ge(S[ready % b], 1)
+            ten.matmul_mx(p[:, BANK * b:BANK * b + NC], cols(q, b, NC), cols(s, b, NC), T.xq[:], T.xs[:],
+                          True, True).then_inc(S[done % b], 1)
+
+    for b in range(G):
+        scal.wait_ge(S["mu%d" % b], 1)
+        scal.activation(cols(T.ru, b, NC), T.pu[:, BANK * b:BANK * b + NC], ActivationFunctionType.Relu,
+                        scale=C).then_inc(S["ru%d" % b], 1)
+
+    mask = topo.mask(core, T.cores[dests[0]])
+    for j in dests:
+        mask &= topo.mask(core, T.cores[j])
+    engines = sum((mask >> e) & 1 for e in range(16))
+    ids = []
+    for j in dests:
+        rid, pid, _ = topo.addr(T.cores[j])
+        ids.append(DstId(rid=rid, pnc=pid))
+    g.wait_ge(S.qh, 1)
+    for view in (cols(T.hq, r, NC).bitcast(dt.uint8), cols(T.hs, r, NC)):
+        g.remote_dma_fused([RemoteDMATransfer(dst_ids=ids, dma_engine_mask=mask, remote_sem=S["arr%d" % r],
+                                              srcs=[view], dsts=[view for _ in dests])], local_sem=S.sent)
+
+    ten.wait_ge(S.qh, 1)
+    ten.wait_ge(S.qw, 1)
+    order = [r] + senders
+    for k, j in enumerate(order):
+        if j != r:
+            ten.wait_ge(S["arr%d" % j], 2 * engines)
+        ten.wait_ge(S["ru%d" % k], 1)
+        ten.matmul_mx(T.pu[:, BANK * k:BANK * k + NC], T.wq[:], T.ws[:], cols(T.hq, j, NC), cols(T.hs, j, NC),
+                      True, True).then_inc(S["my%d" % j], 1)
+    for k, j in enumerate(order):
+        bank, out = T.pu[:, BANK * k:BANK * k + NC], cols(T.yb, j, NC)
+        if k < n - 1:
+            vec.wait_ge(S["my%d" % j], 1)
+            vec.tensor_copy(out, bank).then_inc(S["cy%d" % j], 1)
+            q = sync
+        else:
+            scal.wait_ge(S["my%d" % j], 1)
+            scal.activation(out, bank, ActivationFunctionType.Copy).then_inc(S["cy%d" % j], 1)
+            q = scal
+        q.wait_ge(S["cy%d" % j], 1)
+        q.dma_start(cols(T.y, j, NC), out).then_inc(S["st%d" % j], 16)
+    for k, j in enumerate(order):
+        (sync if k < n - 1 else scal).wait_ge(S["st%d" % j], 16)
+    g.wait_ge(S.sent, 2 * engines)

@@ -24,7 +24,7 @@ SCRATCH = {
     "pu": ("psum", [128, G * BANK], "float32"),
     "pv": ("psum", [128, G * BANK], "float32"),
 }
-SEMAPHORES = (["lx", "lu", "lva", "lvb", "lw", "qx", "qw", "qh", "th", "sent"]
+SEMAPHORES = (["lx", "lua", "lub", "lva", "lvb", "lvc", "lw", "qx", "qw", "qh", "th", "sent"]
               + ["%s%d" % (k, b) for k in ("qu", "qv", "mu", "mv", "ru") for b in range(G)]
               + ["%s%d" % (k, j) for k in ("arr", "my", "cy", "st") for j in range(NR)])
 
@@ -42,14 +42,21 @@ def rank_program(g, core, T, topo):
     sync, scal, vec, ten = g.sync, g.scalar, g.vector, g.tensor
     dests = [(r + k) % n for k in range(1, n)]
     senders = [(r - k) % n for k in range(1, n)]
-    head = (G - 1) * TW
 
-    scal.dma_start(T.ub[:], T.u[:]).then_inc(S.lu, 16)
-    sync.dma_start(T.xb[:], T.x[:]).then_inc(S.lx, 16)
-    sync.dma_start(T.vb[:, 0:head], T.v[:, 0:head]).then_inc(S.lva, 16)
-    sync.dma_start(T.vb[:, head:G * TW], T.v[:, head:G * TW]).then_inc(S.lvb, 16)
-    scal.wait_ge(S.lu, 16)
-    scal.dma_start(T.wb[:], T.w2[:]).then_inc(S.lw, 16)
+    def load(q, buf, src, a, b, sem):
+        q.dma_start(buf[:, TW * a:TW * b], src[:, TW * a:TW * b]).then_inc(S[sem], 16)
+
+    load(sync, T.xb, T.x, 0, 1, "lx")
+    load(scal, T.ub, T.u, 0, 2, "lua")
+    load(sync, T.vb, T.v, 0, 2, "lva")
+    load(scal, T.ub, T.u, 2, 4, "lub")
+    load(sync, T.vb, T.v, 2, 3, "lvb")
+    load(sync, T.vb, T.v, 3, 4, "lvc")
+    scal.wait_ge(S.lx, 16)
+    load(scal, T.wb, T.w2, 0, 1, "lw")
+
+    def pack_u(b):
+        vec.quantize_mx(cols(T.uq, b, NC), cols(T.us, b, NC), cols(T.ub, b, TW)).then_inc(S["qu%d" % b], 1)
 
     def pack_v(b):
         vec.quantize_mx(cols(T.vq, b, NC), cols(T.vs, b, NC), cols(T.vb, b, TW)).then_inc(S["qv%d" % b], 1)
@@ -62,29 +69,34 @@ def rank_program(g, core, T, topo):
 
     vec.wait_ge(S.lx, 16)
     vec.quantize_mx(T.xq[:], T.xs[:], T.xb[:]).then_inc(S.qx, 1)
-    vec.wait_ge(S.lu, 16)
-    for b in range(G):
-        vec.quantize_mx(cols(T.uq, b, NC), cols(T.us, b, NC), cols(T.ub, b, TW)).then_inc(S["qu%d" % b], 1)
+    vec.wait_ge(S.lua, 16)
+    pack_u(0)
+    pack_u(1)
     vec.wait_ge(S.lva, 16)
-    for b in range(G - 1):
-        pack_v(b)
-    for b in range(G - 2):
-        gate(b)
+    pack_v(0)
+    pack_v(1)
+    vec.wait_ge(S.lub, 16)
+    pack_u(2)
+    pack_u(3)
+    gate(0)
     vec.wait_ge(S.lvb, 16)
-    pack_v(G - 1)
-    gate(G - 2)
-    gate(G - 1)
+    pack_v(2)
+    gate(1)
+    vec.wait_ge(S.lvc, 16)
+    pack_v(3)
+    gate(2)
+    gate(3)
     vec.wait_ge(S.th, G)
     vec.quantize_mx(cols(T.hq, r, NC), cols(T.hs, r, NC), T.hb[:]).then_inc(S.qh, 1)
     vec.wait_ge(S.lw, 16)
     vec.quantize_mx(T.wq[:], T.ws[:], T.wb[:]).then_inc(S.qw, 1)
 
     ten.wait_ge(S.qx, 1)
-    for q, s, p, ready, done in ((T.uq, T.us, T.pu, "qu%d", "mu%d"), (T.vq, T.vs, T.pv, "qv%d", "mv%d")):
-        for b in range(G):
-            ten.wait_ge(S[ready % b], 1)
-            ten.matmul_mx(p[:, BANK * b:BANK * b + NC], cols(q, b, NC), cols(s, b, NC), T.xq[:], T.xs[:],
-                          True, True).then_inc(S[done % b], 1)
+    for kind, b in (("u", 0), ("u", 1), ("v", 0), ("v", 1), ("u", 2), ("u", 3), ("v", 2), ("v", 3)):
+        q, s, p = (T.uq, T.us, T.pu) if kind == "u" else (T.vq, T.vs, T.pv)
+        ten.wait_ge(S["q%s%d" % (kind, b)], 1)
+        ten.matmul_mx(p[:, BANK * b:BANK * b + NC], cols(q, b, NC), cols(s, b, NC), T.xq[:], T.xs[:],
+                      True, True).then_inc(S["m%s%d" % (kind, b)], 1)
 
     for b in range(G):
         scal.wait_ge(S["mu%d" % b], 1)

from concourse.bass import DstId, RemoteDMATransfer
from concourse.mybir import dt, AluOpType, ActivationFunctionType

NR = 3
NC = 128
G = 4
TW = 4 * NC
BANK = 512
C = 0.00048828125

SCRATCH = {
    "xb": ("sbuf", [128, TW], "bfloat16"),
    "ub": ("sbuf", [128, G * TW], "bfloat16"),
    "vb": ("sbuf", [128, G * TW], "bfloat16"),
    "wb": ("sbuf", [128, TW], "bfloat16"),
    "hb": ("sbuf", [128, TW], "bfloat16"),
    "xq": ("sbuf", [128, NC], "float8_e4m3fn_x4"), "xs": ("sbuf", [128, NC], "uint8"),
    "uq": ("sbuf", [128, G * NC], "float8_e4m3fn_x4"), "us": ("sbuf", [128, G * NC], "uint8"),
    "vq": ("sbuf", [128, G * NC], "float8_e4m3fn_x4"), "vs": ("sbuf", [128, G * NC], "uint8"),
    "wq": ("sbuf", [128, NC], "float8_e4m3fn_x4"), "ws": ("sbuf", [128, NC], "uint8"),
    "hq": ("sbuf", [128, NR * NC], "float8_e4m3fn_x4"), "hs": ("sbuf", [128, NR * NC], "uint8"),
    "ru": ("sbuf", [128, G * NC], "float32"),
    "yb": ("sbuf", [128, NR * NC], "float32"),
    "pu": ("psum", [128, G * BANK], "float32"),
    "pv": ("psum", [128, G * BANK], "float32"),
}
SEMAPHORES = (["lx", "lua", "lub", "lva", "lvb", "lvc", "lw", "qx", "qw", "qh", "th", "sent"]
              + ["%s%d" % (k, b) for k in ("qu", "qv", "mu", "mv", "ru") for b in range(G)]
              + ["%s%d" % (k, j) for k in ("arr", "my", "cy", "st") for j in range(NR)])


def cols(t, i, w):
    return t[:, w * i:w * i + w]


def rank_program(g, core, T, topo):
    r = T.rank_of(core)
    if r is None:
        return
    S = T.sem
    n = len(T.cores)
    sync, scal, vec, ten = g.sync, g.scalar, g.vector, g.tensor
    dests = [(r + k) % n for k in range(1, n)]
    senders = [(r - k) % n for k in range(1, n)]

    def load(q, buf, src, a, b, sem):
        q.dma_start(buf[:, TW * a:TW * b], src[:, TW * a:TW * b]).then_inc(S[sem], 16)

    load(sync, T.xb, T.x, 0, 1, "lx")
    load(scal, T.ub, T.u, 0, 2, "lua")
    load(sync, T.vb, T.v, 0, 2, "lva")
    load(scal, T.ub, T.u, 2, 4, "lub")
    load(sync, T.vb, T.v, 2, 3, "lvb")
    load(sync, T.vb, T.v, 3, 4, "lvc")
    scal.wait_ge(S.lx, 16)
    load(scal, T.wb, T.w2, 0, 1, "lw")

    def pack_u(b):
        vec.quantize_mx(cols(T.uq, b, NC), cols(T.us, b, NC), cols(T.ub, b, TW)).then_inc(S["qu%d" % b], 1)

    def pack_v(b):
        vec.quantize_mx(cols(T.vq, b, NC), cols(T.vs, b, NC), cols(T.vb, b, TW)).then_inc(S["qv%d" % b], 1)

    def gate(b):
        vec.wait_ge(S["ru%d" % b], 1)
        vec.wait_ge(S["mv%d" % b], 1)
        vec.tensor_tensor(T.hb[:, b:TW:G], cols(T.ru, b, NC), T.pv[:, BANK * b:BANK * b + NC],
                          AluOpType.mult).then_inc(S.th, 1)

    vec.wait_ge(S.lx, 16)
    vec.quantize_mx(T.xq[:], T.xs[:], T.xb[:]).then_inc(S.qx, 1)
    vec.wait_ge(S.lua, 16)
    pack_u(0)
    pack_u(1)
    vec.wait_ge(S.lva, 16)
    pack_v(0)
    pack_v(1)
    vec.wait_ge(S.lub, 16)
    pack_u(2)
    pack_u(3)
    gate(0)
    vec.wait_ge(S.lvb, 16)
    pack_v(2)
    gate(1)
    vec.wait_ge(S.lvc, 16)
    pack_v(3)
    gate(2)
    gate(3)
    vec.wait_ge(S.th, G)
    vec.quantize_mx(cols(T.hq, r, NC), cols(T.hs, r, NC), T.hb[:]).then_inc(S.qh, 1)
    vec.wait_ge(S.lw, 16)
    vec.quantize_mx(T.wq[:], T.ws[:], T.wb[:]).then_inc(S.qw, 1)

    ten.wait_ge(S.qx, 1)
    for kind, b in (("u", 0), ("u", 1), ("v", 0), ("v", 1), ("u", 2), ("u", 3), ("v", 2), ("v", 3)):
        q, s, p = (T.uq, T.us, T.pu) if kind == "u" else (T.vq, T.vs, T.pv)
        ten.wait_ge(S["q%s%d" % (kind, b)], 1)
        ten.matmul_mx(p[:, BANK * b:BANK * b + NC], cols(q, b, NC), cols(s, b, NC), T.xq[:], T.xs[:],
                      True, True).then_inc(S["m%s%d" % (kind, b)], 1)

    for b in range(G):
        scal.wait_ge(S["mu%d" % b], 1)
        scal.activation(cols(T.ru, b, NC), T.pu[:, BANK * b:BANK * b + NC], ActivationFunctionType.Relu,
                        scale=C).then_inc(S["ru%d" % b], 1)

    mask = topo.mask(core, T.cores[dests[0]])
    for j in dests:
        mask &= topo.mask(core, T.cores[j])
    engines = sum((mask >> e) & 1 for e in range(16))
    ids = []
    for j in dests:
        rid, pid, _ = topo.addr(T.cores[j])
        ids.append(DstId(rid=rid, pnc=pid))
    g.wait_ge(S.qh, 1)
    for view in (cols(T.hq, r, NC).bitcast(dt.uint8), cols(T.hs, r, NC)):
        g.remote_dma_fused([RemoteDMATransfer(dst_ids=ids, dma_engine_mask=mask, remote_sem=S["arr%d" % r],
                                              srcs=[view], dsts=[view for _ in dests])], local_sem=S.sent)

    ten.wait_ge(S.qh, 1)
    ten.wait_ge(S.qw, 1)
    order = [r] + senders
    for k, j in enumerate(order):
        if j != r:
            ten.wait_ge(S["arr%d" % j], 2 * engines)
        ten.wait_ge(S["ru%d" % k], 1)
        ten.matmul_mx(T.pu[:, BANK * k:BANK * k + NC], T.wq[:], T.ws[:], cols(T.hq, j, NC), cols(T.hs, j, NC),
                      True, True).then_inc(S["my%d" % j], 1)
    for k, j in enumerate(order):
        bank, out = T.pu[:, BANK * k:BANK * k + NC], cols(T.yb, j, NC)
        if k < n - 1:
            vec.wait_ge(S["my%d" % j], 1)
            vec.tensor_copy(out, bank).then_inc(S["cy%d" % j], 1)
            q = sync
        else:
            scal.wait_ge(S["my%d" % j], 1)
            scal.activation(out, bank, ActivationFunctionType.Copy).then_inc(S["cy%d" % j], 1)
            q = scal
        q.wait_ge(S["cy%d" % j], 1)
        q.dma_start(cols(T.y, j, NC), out).then_inc(S["st%d" % j], 16)
    for k, j in enumerate(order):
        (sync if k < n - 1 else scal).wait_ge(S["st%d" % j], 16)
    g.wait_ge(S.sent, 2 * engines)
